import numpy as np
import ml_dtypes


def mxq(x, axis, fmt="e4m3"):
    dtype, down = {"e4m3": (ml_dtypes.float8_e4m3fn, 7), "e5m2": (ml_dtypes.float8_e5m2, 14)}[fmt]
    v = np.moveaxis(np.asarray(x, np.float32).astype(ml_dtypes.bfloat16).astype(np.float64), axis, -1)
    blocks = v.reshape(v.shape[:-1] + (-1, 32))
    amax = np.abs(blocks).max(-1, keepdims=True)
    byte = np.maximum(np.where(amax > 0, np.frexp(amax)[1] - 1 + 127, 0) - down, 1)
    scale = np.exp2(byte - 127.0)
    codes = (blocks / scale).astype(np.float32).astype(dtype).astype(np.float64)
    return np.moveaxis((codes * scale).reshape(v.shape), -1, axis)


WIDE = False


def mx_kscale(k):
    if not WIDE:
        return np.ones(k)
    levels = np.array([30, -30])
    if k % 512:
        return np.exp2(np.random.permutation(np.resize(levels, k // 32))).repeat(32)
    a = np.empty((k // 512, 16))
    for p in range(k // 512):
        a[p, :8] = np.random.permutation(np.resize(levels, 8))
        for g in range(8):
            far = levels[np.abs(levels - a[p, g]) >= 10]
            a[p, g + 8] = far[np.random.randint(len(far))]
    return np.exp2(a.ravel()).repeat(32)


def f64(x):
    return np.asarray(x).astype(np.float64)


def striped(idx):
    return np.tile(np.asarray(idx).reshape(-1, 16).T, (8, 1)).astype(np.uint16)


def unstriped(offs):
    return offs[:16].T.reshape(-1).astype(np.int64)


K, T, J, I, S, V = 1024, 1024, 256, 256, 512, 1024


def setup_inputs():
    n = np.random.standard_normal
    idx = np.random.permutation(T)[:J]
    idx2 = np.random.permutation(S)[:J]
    idx3 = np.random.permutation(V)[:I]
    fk = mx_kscale(K)
    return {
        "xf": (n((K, T)) * 0.03).astype(np.float32),
        "xb": (n((K, S))).astype(np.float32),
        "fk": (np.random.uniform(0.5, 2.0, (K, 1)) * fk[:, None]).astype(np.float32),
        "kf": (n((K, V))).astype(np.float32),
        "ko": (n((K, I)) * 0.6).astype(np.float32),
        "fi": (np.random.uniform(0.5, 2.0, (K, 1)) / fk[:, None]).astype(np.float32),
        "bi": (np.random.uniform(-0.7, 0.7, (1, I))).astype(np.float32),
        "pr": (np.random.uniform(0.5, 1.5, (1, I))).astype(np.float32),
        "offs": striped(idx),
        "offs2": striped(idx2),
        "offs3": striped(idx3),
    }


def reference(xf, xb, fk, kf, ko, fi, bi, pr, offs, offs2, offs3):
    idx = unstriped(offs)
    idx2 = unstriped(offs2)
    idx3 = unstriped(offs3)
    u = f64(xf)[:, idx] * f64(xb)[:, idx2] * f64(fk)
    vk = (f64(kf)[:, idx3] + f64(ko)) * f64(fi)
    uq = mxq(u, 0, "e5m2")
    vkq = mxq(vk, 0, "e5m2")
    a0 = uq.T @ vkq
    a = a0 + f64(bi)
    e = np.exp(0.7 * a) * f64(pr)
    y = 256.0 * e / np.sum(e, axis=1, keepdims=True) - f64(pr)
    return y

@@ -1,0 +1,166 @@
+from contextlib import ExitStack
+
+import concourse.mybir as mybir
+from concourse.masks import make_identity
+
+K, T, J, I, S, V = 1024, 1024, 256, 256, 512, 1024
+FLOPS = 2 * K * J * I
+
+F32 = mybir.dt.float32
+BF16 = mybir.dt.bfloat16
+U32 = mybir.dt.uint32
+U16 = mybir.dt.uint16
+U8 = mybir.dt.uint8
+E5M2X4 = mybir.dt.float8_e5m2_x4
+ALU = mybir.AluOpType
+ACT = mybir.ActivationFunctionType
+
+P = 128
+PACK = 4
+PASSES = K // (P * PACK)
+HALVES = J // P
+LIST_COLS = J // 16
+
+
+def tile_list_scores_products_mixed_shares_f_kernel(tc, xf, xb, fk, kf, ko, fi, bi, pr, offs, offs2, offs3, out):
+    nc = tc.nc
+    with ExitStack() as ctx:
+        lists = ctx.enter_context(tc.tile_pool(name="lists", bufs=1))
+        sb = ctx.enter_context(tc.tile_pool(name="sb", bufs=1))
+        ps = ctx.enter_context(tc.psum_pool(name="ps", bufs=1))
+
+        def rows(x):
+            return x.rearrange("(a p t) w -> a p t w", p=P, t=PACK)
+
+        idx = lists.tile([P, LIST_COLS], U16, name="idx")
+        idx2 = lists.tile([P, LIST_COLS], U16, name="idx2")
+        idx3 = lists.tile([P, LIST_COLS], U16, name="idx3")
+
+        ko_sb = sb.tile([P, PASSES, PACK, I], F32, name="ko_sb")
+        xb_sb = [sb.tile([P, PACK, S], F32, name="xb_sb%d" % a) for a in range(PASSES)]
+        kf_sb = [sb.tile([P, PACK, V], F32, name="kf_sb%d" % a) for a in range(PASSES)]
+        xf_first = [sb.tile([P, 2, T], F32, name="xf_first%d" % h) for h in range(2)]
+        xf_last = [sb.tile([P, T], F32, name="xf_last%d" % t) for t in range(PACK)]
+
+        fk_sb = sb.tile([P, PASSES, PACK], F32, name="fk_sb")
+        fi_sb = sb.tile([P, PASSES, PACK], F32, name="fi_sb")
+        bi_col = sb.tile([P, 2], F32, name="bi_col")
+        pr_col = sb.tile([P, 2], F32, name="pr_col")
+
+        nc.sync.dma_start(ko_sb[:], ko.rearrange("(a p t) w -> p a t w", p=P, t=PACK))
+        nc.sync.dma_start(idx2[:], offs2)
+        nc.sync.dma_start(xb_sb[0][:], rows(xb)[0])
+        nc.sync.dma_start(idx3[:], offs3)
+        nc.sync.dma_start(idx[:], offs)
+        nc.sync.dma_start(xb_sb[1][:], rows(xb)[1])
+        nc.sync.dma_start(fi_sb[:], fi.rearrange("(a p t) o -> p a (t o)", p=P, t=PACK))
+        nc.sync.dma_start(fk_sb[:], fk.rearrange("(a p t) o -> p a (t o)", p=P, t=PACK))
+        nc.sync.dma_start(kf_sb[0][:], rows(kf)[0])
+        nc.sync.dma_start(bi_col[:], bi.rearrange("o (p c) -> (o p) c", c=2))
+        nc.sync.dma_start(pr_col[:], pr.rearrange("o (p c) -> (o p) c", c=2))
+        nc.sync.dma_start(kf_sb[1][:], rows(kf)[1])
+        for h in range(2):
+            nc.sync.dma_start(xf_first[h][:], rows(xf)[0, :, 2 * h : 2 * h + 2, :])
+        for t in range(PACK):
+            nc.sync.dma_start(xf_last[t][:], rows(xf)[1, :, t, :])
+
+        ident = sb.tile([P, P], F32, name="ident")
+        make_identity(nc, ident[:])
+        bi_ps = ps.tile([P, 2, P], F32, name="bi_ps")
+        pr_ps = ps.tile([P, 2, P], F32, name="pr_ps")
+        for c in range(2):
+            nc.tensor.transpose(bi_ps[:, c, :], bi_col[:, c : c + 1].to_broadcast([P, P]), ident[:])
+        for c in range(2):
+            nc.tensor.transpose(pr_ps[:, c, :], pr_col[:, c : c + 1].to_broadcast([P, P]), ident[:])
+        bias_neg = sb.tile([P, I], F32, name="bias_neg")
+        prior = sb.tile([P, I], F32, name="prior")
+        nc.vector.tensor_scalar(
+            bias_neg[:].rearrange("p (q c) -> p q c", c=2), bi_ps[:].rearrange("p c q -> p q c"), -0.7, None, ALU.mult
+        )
+        nc.vector.tensor_copy(prior[:].rearrange("p (q c) -> p q c", c=2), pr_ps[:].rearrange("p c q -> p q c"))
+
+        def quantise(name, words, width):
+            codes = sb.tile([P, width], U32, name=name + "_codes", align_bytes=64)
+            scales = sb.tile([P, width], U8, name=name + "_scales", align_bytes=64)
+            nc.vector.quantize_mx(
+                out=codes[:].bitcast(E5M2X4), scales=scales[:], in_=words[:].rearrange("p w t -> p (w t)")
+            )
+            return codes, scales
+
+        xb_g = []
+        for a in range(PASSES):
+            g = sb.tile([P, PACK, J], F32, name="xb_g%d" % a)
+            for t in range(PACK):
+                nc.scalar.activation(g[:, t, :], xb_sb[a][:, t, :].indirect(idx2[:]), ACT.Copy)
+            xb_g.append(g)
+
+        vk_q = []
+        for a in range(PASSES):
+            words = sb.tile([P, I, PACK], BF16, name="vk_words%d" % a, align_bytes=64)
+            for t in range(PACK):
+                g = sb.tile([P, I], F32, name="kf_g%d_%d" % (a, t))
+                nc.scalar.activation(g[:], kf_sb[a][:, t, :].indirect(idx3[:]), ACT.Copy)
+                keys = sb.tile([P, I], F32, name="keys%d_%d" % (a, t))
+                nc.vector.tensor_tensor(keys[:], g[:], ko_sb[:, a, t, :], ALU.add)
+                nc.vector.tensor_scalar(words[:, :, t], keys[:], fi_sb[:, a, t : t + 1], None, ALU.mult)
+            vk_q.append(quantise("vk%d" % a, words, I))
+
+        scores = [ps.tile([P, I], F32, name="scores%d" % h) for h in range(HALVES)]
+
+        def multiply(h, a, u_codes, u_scales):
+            nc.tensor.matmul_mx(
+                out=scores[h][:],
+                lhsT=u_codes.bitcast(E5M2X4),
+                lhsT_scale=u_scales,
+                rhs=vk_q[a][0][:].bitcast(E5M2X4),
+                rhs_scale=vk_q[a][1][:],
+                start=(a == 0),
+                stop=(a == PASSES - 1),
+            )
+
+        words = sb.tile([P, J, PACK], BF16, name="u_words0", align_bytes=64)
+        for t in range(PACK):
+            g = sb.tile([P, J], F32, name="xf_g%d" % t)
+            nc.scalar.activation(g[:], xf_first[t // 2][:, t % 2, :].indirect(idx[:]), ACT.Copy)
+            prod = sb.tile([P, J], F32, name="prod0_%d" % t)
+            nc.vector.tensor_tensor(prod[:], g[:], xb_g[0][:, t, :], ALU.mult)
+            nc.vector.tensor_scalar(words[:, :, t], prod[:], fk_sb[:, 0, t : t + 1], None, ALU.mult)
+        u_codes, u_scales = quantise("u0", words, J)
+        for h in range(HALVES):
+            multiply(h, 0, u_codes[:, h * P : (h + 1) * P], u_scales[:, h * P : (h + 1) * P])
+
+        half_words = [sb.tile([P, P, PACK], BF16, name="u_words1_%d" % h, align_bytes=64) for h in range(HALVES)]
+        for t in range(PACK):
+            prods = []
+            for h in range(HALVES):
+                prod = sb.tile([P, P], F32, name="prod1_%d_%d" % (t, h))
+                picks = idx[:, h * (P // 16) : (h + 1) * (P // 16)]
+                nc.vector.tensor_tensor(
+                    prod[:], xf_last[t][:].indirect(picks), xb_g[1][:, t, h * P : (h + 1) * P], ALU.mult
+                )
+                prods.append(prod)
+            for h in range(HALVES):
+                nc.vector.tensor_scalar(half_words[h][:, :, t], prods[h][:], fk_sb[:, 1, t : t + 1], None, ALU.mult)
+        for h in range(HALVES):
+            u_codes, u_scales = quantise("u1_%d" % h, half_words[h], P)
+            multiply(h, 1, u_codes[:], u_scales[:])
+
+        neg, low, ex, e, total, inv, y = [], [], [], [], [], [], []
+        for h in range(HALVES):
+            neg.append(sb.tile([P, I], F32, name="neg%d" % h))
+            low.append(sb.tile([P, 1], F32, name="low%d" % h))
+            ex.append(sb.tile([P, I], F32, name="ex%d" % h))
+            e.append(sb.tile([P, I], F32, name="e%d" % h))
+            total.append(sb.tile([P, 1], F32, name="total%d" % h))
+            inv.append(sb.tile([P, 2], F32, name="inv%d" % h))
+            y.append(sb.tile([P, I], F32, name="y%d" % h))
+        for h in range(HALVES):
+            nc.vector.scalar_tensor_tensor(neg[h][:], scores[h][:], -0.7, bias_neg[:], ALU.mult, ALU.add)
+            nc.vector.tensor_reduce(low[h][:], neg[h][:], mybir.AxisListType.X, ALU.min)
+            nc.scalar.activation(ex[h][:], neg[h][:], ACT.Exp, bias=low[h][:], scale=-1.0)
+        for h in range(HALVES):
+            nc.vector.scalar_tensor_tensor(e[h][:], ex[h][:], 1.0, prior[:], ALU.mult, ALU.mult, accum_out=total[h][:])
+            nc.vector.reciprocal(inv[h][:, 0:1], total[h][:])
+            nc.vector.tensor_scalar(inv[h][:, 1:2], inv[h][:, 0:1], 256.0, None, ALU.mult)
+            nc.vector.scalar_tensor_tensor(y[h][:], e[h][:], inv[h][:, 1:2], prior[:], ALU.mult, ALU.subtract)
+            nc.sync.dma_start(out[h * P : (h + 1) * P, :], y[h][:])

@@ -38,31 +38,32 @@ def tile_list_scores_products_mixed_shares_f_kernel(tc, xf, xb, fk, kf, ko, fi, 
 
         ko_sb = sb.tile([P, PASSES, PACK, I], F32, name="ko_sb")
         xb_sb = [sb.tile([P, PACK, S], F32, name="xb_sb%d" % a) for a in range(PASSES)]
-        kf_sb = [sb.tile([P, PACK, V], F32, name="kf_sb%d" % a) for a in range(PASSES)]
-        xf_first = [sb.tile([P, 2, T], F32, name="xf_first%d" % h) for h in range(2)]
-        xf_last = [sb.tile([P, T], F32, name="xf_last%d" % t) for t in range(PACK)]
+        kf_first = sb.tile([P, PACK, V], F32, name="kf_first")
+        kf_last = [sb.tile([P, 2, V], F32, name="kf_last%d" % c) for c in range(2)]
+        xf_sb = [[sb.tile([P, T], F32, name="xf_sb%d_%d" % (a, t)) for t in range(PACK)] for a in range(PASSES)]
 
         fk_sb = sb.tile([P, PASSES, PACK], F32, name="fk_sb")
         fi_sb = sb.tile([P, PASSES, PACK], F32, name="fi_sb")
         bi_col = sb.tile([P, 2], F32, name="bi_col")
         pr_col = sb.tile([P, 2], F32, name="pr_col")
 
-        nc.sync.dma_start(ko_sb[:], ko.rearrange("(a p t) w -> p a t w", p=P, t=PACK))
+        nc.scalar.dma_start(fi_sb[:], fi.rearrange("(a p t) o -> p a (t o)", p=P, t=PACK))
+        nc.scalar.dma_start(fk_sb[:], fk.rearrange("(a p t) o -> p a (t o)", p=P, t=PACK))
+        nc.scalar.dma_start(bi_col[:], bi.rearrange("o (p c) -> (o p) c", c=2))
+        nc.scalar.dma_start(pr_col[:], pr.rearrange("o (p c) -> (o p) c", c=2))
+
+        nc.sync.dma_start(kf_first[:], rows(kf)[0])
+        nc.sync.dma_start(idx3[:], offs3)
         nc.sync.dma_start(idx2[:], offs2)
         nc.sync.dma_start(xb_sb[0][:], rows(xb)[0])
-        nc.sync.dma_start(idx3[:], offs3)
+        nc.sync.dma_start(ko_sb[:], ko.rearrange("(a p t) w -> p a t w", p=P, t=PACK))
         nc.sync.dma_start(idx[:], offs)
+        for c in range(2):
+            nc.sync.dma_start(kf_last[c][:], rows(kf)[1, :, 2 * c : 2 * c + 2, :])
         nc.sync.dma_start(xb_sb[1][:], rows(xb)[1])
-        nc.sync.dma_start(fi_sb[:], fi.rearrange("(a p t) o -> p a (t o)", p=P, t=PACK))
-        nc.sync.dma_start(fk_sb[:], fk.rearrange("(a p t) o -> p a (t o)", p=P, t=PACK))
-        nc.sync.dma_start(kf_sb[0][:], rows(kf)[0])
-        nc.sync.dma_start(bi_col[:], bi.rearrange("o (p c) -> (o p) c", c=2))
-        nc.sync.dma_start(pr_col[:], pr.rearrange("o (p c) -> (o p) c", c=2))
-        nc.sync.dma_start(kf_sb[1][:], rows(kf)[1])
-        for h in range(2):
-            nc.sync.dma_start(xf_first[h][:], rows(xf)[0, :, 2 * h : 2 * h + 2, :])
-        for t in range(PACK):
-            nc.sync.dma_start(xf_last[t][:], rows(xf)[1, :, t, :])
+        for a in range(PASSES):
+            for t in range(PACK):
+                nc.sync.dma_start(xf_sb[a][t][:], rows(xf)[a, :, t, :])
 
         ident = sb.tile([P, P], F32, name="ident")
         make_identity(nc, ident[:])
@@ -87,23 +88,26 @@ def tile_list_scores_products_mixed_shares_f_kernel(tc, xf, xb, fk, kf, ko, fi, 
             )
             return codes, scales
 
-        xb_g = []
-        for a in range(PASSES):
+        def gather_xb(a):
             g = sb.tile([P, PACK, J], F32, name="xb_g%d" % a)
             for t in range(PACK):
                 nc.scalar.activation(g[:, t, :], xb_sb[a][:, t, :].indirect(idx2[:]), ACT.Copy)
-            xb_g.append(g)
+            return g
 
-        vk_q = []
-        for a in range(PASSES):
+        def make_vk(a, windows):
             words = sb.tile([P, I, PACK], BF16, name="vk_words%d" % a, align_bytes=64)
             for t in range(PACK):
                 g = sb.tile([P, I], F32, name="kf_g%d_%d" % (a, t))
-                nc.scalar.activation(g[:], kf_sb[a][:, t, :].indirect(idx3[:]), ACT.Copy)
+                nc.scalar.activation(g[:], windows[t].indirect(idx3[:]), ACT.Copy)
                 keys = sb.tile([P, I], F32, name="keys%d_%d" % (a, t))
                 nc.vector.tensor_tensor(keys[:], g[:], ko_sb[:, a, t, :], ALU.add)
                 nc.vector.tensor_scalar(words[:, :, t], keys[:], fi_sb[:, a, t : t + 1], None, ALU.mult)
-            vk_q.append(quantise("vk%d" % a, words, I))
+            return quantise("vk%d" % a, words, I)
+
+        vk_q = [make_vk(0, [kf_first[:, t, :] for t in range(PACK)])]
+        xb_g = [gather_xb(0)]
+        vk_q.append(make_vk(1, [kf_last[t // 2][:, t % 2, :] for t in range(PACK)]))
+        xb_g.append(gather_xb(1))
 
         scores = [ps.tile([P, I], F32, name="scores%d" % h) for h in range(HALVES)]
 
@@ -118,49 +122,45 @@ def tile_list_scores_products_mixed_shares_f_kernel(tc, xf, xb, fk, kf, ko, fi, 
                 stop=(a == PASSES - 1),
             )
 
-        words = sb.tile([P, J, PACK], BF16, name="u_words0", align_bytes=64)
-        for t in range(PACK):
-            g = sb.tile([P, J], F32, name="xf_g%d" % t)
-            nc.scalar.activation(g[:], xf_first[t // 2][:, t % 2, :].indirect(idx[:]), ACT.Copy)
-            prod = sb.tile([P, J], F32, name="prod0_%d" % t)
-            nc.vector.tensor_tensor(prod[:], g[:], xb_g[0][:, t, :], ALU.mult)
-            nc.vector.tensor_scalar(words[:, :, t], prod[:], fk_sb[:, 0, t : t + 1], None, ALU.mult)
-        u_codes, u_scales = quantise("u0", words, J)
-        for h in range(HALVES):
-            multiply(h, 0, u_codes[:, h * P : (h + 1) * P], u_scales[:, h * P : (h + 1) * P])
-
-        half_words = [sb.tile([P, P, PACK], BF16, name="u_words1_%d" % h, align_bytes=64) for h in range(HALVES)]
-        for t in range(PACK):
-            prods = []
+        for a in range(PASSES):
+            half_words = [
+                sb.tile([P, P, PACK], BF16, name="u_words%d_%d" % (a, h), align_bytes=64) for h in range(HALVES)
+            ]
+            for t in range(PACK):
+                prod = sb.tile([P, J], F32, name="prod%d_%d" % (a, t))
+                pieces = HALVES if (a, t) == (PASSES - 1, PACK - 1) else 1
+                width = J // pieces
+                for c in range(pieces):
+                    cols = slice(c * width, (c + 1) * width)
+                    picks = idx[:, c * width // 16 : (c + 1) * width // 16]
+                    nc.vector.tensor_tensor(prod[:, cols], xf_sb[a][t][:].indirect(picks), xb_g[a][:, t, cols], ALU.mult)
+                for h in range(HALVES):
+                    nc.scalar.activation(
+                        half_words[h][:, :, t], prod[:, h * P : (h + 1) * P], ACT.Copy, scale=fk_sb[:, a, t : t + 1]
+                    )
             for h in range(HALVES):
-                prod = sb.tile([P, P], F32, name="prod1_%d_%d" % (t, h))
-                picks = idx[:, h * (P // 16) : (h + 1) * (P // 16)]
-                nc.vector.tensor_tensor(
-                    prod[:], xf_last[t][:].indirect(picks), xb_g[1][:, t, h * P : (h + 1) * P], ALU.mult
-                )
-                prods.append(prod)
-            for h in range(HALVES):
-                nc.vector.tensor_scalar(half_words[h][:, :, t], prods[h][:], fk_sb[:, 1, t : t + 1], None, ALU.mult)
-        for h in range(HALVES):
-            u_codes, u_scales = quantise("u1_%d" % h, half_words[h], P)
-            multiply(h, 1, u_codes[:], u_scales[:])
+                u_codes, u_scales = quantise("u%d_%d" % (a, h), half_words[h], P)
+                multiply(h, a, u_codes[:], u_scales[:])
 
-        neg, low, ex, e, total, inv, y = [], [], [], [], [], [], []
-        for h in range(HALVES):
-            neg.append(sb.tile([P, I], F32, name="neg%d" % h))
-            low.append(sb.tile([P, 1], F32, name="low%d" % h))
-            ex.append(sb.tile([P, I], F32, name="ex%d" % h))
-            e.append(sb.tile([P, I], F32, name="e%d" % h))
-            total.append(sb.tile([P, 1], F32, name="total%d" % h))
-            inv.append(sb.tile([P, 2], F32, name="inv%d" % h))
-            y.append(sb.tile([P, I], F32, name="y%d" % h))
+        neg = [sb.tile([P, I], F32, name="neg%d" % h) for h in range(HALVES)]
+        low = [sb.tile([P, 1], F32, name="low%d" % h) for h in range(HALVES)]
+        ex = [sb.tile([P, I], F32, name="ex%d" % h) for h in range(HALVES)]
+        e = [sb.tile([P, I], F32, name="e%d" % h) for h in range(HALVES)]
+        y = [sb.tile([P, I], F32, name="y%d" % h) for h in range(HALVES)]
+        total = sb.tile([P, HALVES], F32, name="total")
+        inverse = sb.tile([P, HALVES], F32, name="inverse")
+        share = sb.tile([P, HALVES], F32, name="share")
         for h in range(HALVES):
             nc.vector.scalar_tensor_tensor(neg[h][:], scores[h][:], -0.7, bias_neg[:], ALU.mult, ALU.add)
+        for h in range(HALVES):
             nc.vector.tensor_reduce(low[h][:], neg[h][:], mybir.AxisListType.X, ALU.min)
             nc.scalar.activation(ex[h][:], neg[h][:], ACT.Exp, bias=low[h][:], scale=-1.0)
         for h in range(HALVES):
-            nc.vector.scalar_tensor_tensor(e[h][:], ex[h][:], 1.0, prior[:], ALU.mult, ALU.mult, accum_out=total[h][:])
-            nc.vector.reciprocal(inv[h][:, 0:1], total[h][:])
-            nc.vector.tensor_scalar(inv[h][:, 1:2], inv[h][:, 0:1], 256.0, None, ALU.mult)
-            nc.vector.scalar_tensor_tensor(y[h][:], e[h][:], inv[h][:, 1:2], prior[:], ALU.mult, ALU.subtract)
+            nc.vector.scalar_tensor_tensor(
+                e[h][:], ex[h][:], 1.0, prior[:], ALU.mult, ALU.mult, accum_out=total[:, h : h + 1]
+            )
+        nc.vector.reciprocal(inverse[:], total[:])
+        nc.vector.tensor_scalar(share[:], inverse[:], 256.0, None, ALU.mult)
+        for h in range(HALVES):
+            nc.vector.scalar_tensor_tensor(y[h][:], e[h][:], share[:, h : h + 1], prior[:], ALU.mult, ALU.subtract)
             nc.sync.dma_start(out[h * P : (h + 1) * P, :], y[h][:])

@@ -20,6 +20,7 @@ PACK = 4
 PASSES = K // (P * PACK)
 HALVES = J // P
 LIST_COLS = J // 16
+FK_ROW, FI_ROW, COL_ROW, SMALL_ROWS = 0, 2, 4, 5
 
 
 def tile_list_scores_products_mixed_shares_f_kernel(tc, xf, xb, fk, kf, ko, fi, bi, pr, offs, offs2, offs3, out):
@@ -42,15 +43,12 @@ def tile_list_scores_products_mixed_shares_f_kernel(tc, xf, xb, fk, kf, ko, fi, 
         kf_last = [sb.tile([P, 2, V], F32, name="kf_last%d" % c) for c in range(2)]
         xf_sb = [[sb.tile([P, T], F32, name="xf_sb%d_%d" % (a, t)) for t in range(PACK)] for a in range(PASSES)]
 
-        fk_sb = sb.tile([P, PASSES, PACK], F32, name="fk_sb")
-        fi_sb = sb.tile([P, PASSES, PACK], F32, name="fi_sb")
-        bi_col = sb.tile([P, 2], F32, name="bi_col")
-        pr_col = sb.tile([P, 2], F32, name="pr_col")
-
-        nc.scalar.dma_start(fi_sb[:], fi.rearrange("(a p t) o -> p a (t o)", p=P, t=PACK))
-        nc.scalar.dma_start(fk_sb[:], fk.rearrange("(a p t) o -> p a (t o)", p=P, t=PACK))
-        nc.scalar.dma_start(bi_col[:], bi.rearrange("o (p c) -> (o p) c", c=2))
-        nc.scalar.dma_start(pr_col[:], pr.rearrange("o (p c) -> (o p) c", c=2))
+        small = sb.tile([P, P * PACK], F32, name="small")
+        nc.vector.memset(small[:], 0.0)
+        nc.scalar.dma_start(small[FK_ROW : FK_ROW + PASSES, :], fk.rearrange("(a r) o -> a (r o)", a=PASSES))
+        nc.scalar.dma_start(small[FI_ROW : FI_ROW + PASSES, :], fi.rearrange("(a r) o -> a (r o)", a=PASSES))
+        nc.scalar.dma_start(small[COL_ROW : COL_ROW + 1, 0:I], bi)
+        nc.scalar.dma_start(small[COL_ROW : COL_ROW + 1, I : 2 * I], pr)
 
         nc.sync.dma_start(kf_first[:], rows(kf)[0])
         nc.sync.dma_start(idx3[:], offs3)
@@ -67,18 +65,21 @@ def tile_list_scores_products_mixed_shares_f_kernel(tc, xf, xb, fk, kf, ko, fi, 
 
         ident = sb.tile([P, P], F32, name="ident")
         make_identity(nc, ident[:])
-        bi_ps = ps.tile([P, 2, P], F32, name="bi_ps")
-        pr_ps = ps.tile([P, 2, P], F32, name="pr_ps")
-        for c in range(2):
-            nc.tensor.transpose(bi_ps[:, c, :], bi_col[:, c : c + 1].to_broadcast([P, P]), ident[:])
-        for c in range(2):
-            nc.tensor.transpose(pr_ps[:, c, :], pr_col[:, c : c + 1].to_broadcast([P, P]), ident[:])
+        turned_ps = ps.tile([P, PACK, P], F32, name="turned_ps")
+        for t in range(PACK):
+            nc.tensor.transpose(turned_ps[:, t, :], small[:, t :: PACK], ident[:])
+        turned = sb.tile([P, PACK, SMALL_ROWS], F32, name="turned")
+        nc.vector.tensor_copy(turned[:], turned_ps[:, :, 0:SMALL_ROWS])
+        spread_ps = ps.tile([P, PACK, P], F32, name="spread_ps")
+        for t in range(PACK):
+            nc.tensor.transpose(spread_ps[:, t, :], turned[:, t, COL_ROW : COL_ROW + 1].to_broadcast([P, P]), ident[:])
         bias_neg = sb.tile([P, I], F32, name="bias_neg")
         prior = sb.tile([P, I], F32, name="prior")
+        by_column = spread_ps[:].rearrange("p t q -> p q t")
         nc.vector.tensor_scalar(
-            bias_neg[:].rearrange("p (q c) -> p q c", c=2), bi_ps[:].rearrange("p c q -> p q c"), -0.7, None, ALU.mult
+            bias_neg[:].rearrange("p (q t) -> p q t", t=PACK), by_column[:, 0 : I // PACK, :], -0.7, None, ALU.mult
         )
-        nc.vector.tensor_copy(prior[:].rearrange("p (q c) -> p q c", c=2), pr_ps[:].rearrange("p c q -> p q c"))
+        nc.vector.tensor_copy(prior[:].rearrange("p (q t) -> p q t", t=PACK), by_column[:, I // PACK : P, :])
 
         def quantise(name, words, width):
             codes = sb.tile([P, width], U32, name=name + "_codes", align_bytes=64)
@@ -101,7 +102,7 @@ def tile_list_scores_products_mixed_shares_f_kernel(tc, xf, xb, fk, kf, ko, fi, 
                 nc.scalar.activation(g[:], windows[t].indirect(idx3[:]), ACT.Copy)
                 keys = sb.tile([P, I], F32, name="keys%d_%d" % (a, t))
                 nc.vector.tensor_tensor(keys[:], g[:], ko_sb[:, a, t, :], ALU.add)
-                nc.vector.tensor_scalar(words[:, :, t], keys[:], fi_sb[:, a, t : t + 1], None, ALU.mult)
+                nc.vector.tensor_scalar(words[:, :, t], keys[:], turned[:, t, FI_ROW + a : FI_ROW + a + 1], None, ALU.mult)
             return quantise("vk%d" % a, words, I)
 
         vk_q = [make_vk(0, [kf_first[:, t, :] for t in range(PACK)])]
@@ -136,7 +137,7 @@ def tile_list_scores_products_mixed_shares_f_kernel(tc, xf, xb, fk, kf, ko, fi, 
                     nc.vector.tensor_tensor(prod[:, cols], xf_sb[a][t][:].indirect(picks), xb_g[a][:, t, cols], ALU.mult)
                 for h in range(HALVES):
                     nc.scalar.activation(
-                        half_words[h][:, :, t], prod[:, h * P : (h + 1) * P], ACT.Copy, scale=fk_sb[:, a, t : t + 1]
+                        half_words[h][:, :, t], prod[:, h * P : (h + 1) * P], ACT.Copy, scale=turned[:, t, FK_ROW + a : FK_ROW + a + 1]
                     )
             for h in range(HALVES):
                 u_codes, u_scales = quantise("u%d_%d" % (a, h), half_words[h], P)
@@ -147,20 +148,18 @@ def tile_list_scores_products_mixed_shares_f_kernel(tc, xf, xb, fk, kf, ko, fi, 
         ex = [sb.tile([P, I], F32, name="ex%d" % h) for h in range(HALVES)]
         e = [sb.tile([P, I], F32, name="e%d" % h) for h in range(HALVES)]
         y = [sb.tile([P, I], F32, name="y%d" % h) for h in range(HALVES)]
-        total = sb.tile([P, HALVES], F32, name="total")
-        inverse = sb.tile([P, HALVES], F32, name="inverse")
-        share = sb.tile([P, HALVES], F32, name="share")
+        total = [sb.tile([P, 1], F32, name="total%d" % h) for h in range(HALVES)]
+        inverse = [sb.tile([P, 1], F32, name="inverse%d" % h) for h in range(HALVES)]
+        share = [sb.tile([P, 1], F32, name="share%d" % h) for h in range(HALVES)]
         for h in range(HALVES):
             nc.vector.scalar_tensor_tensor(neg[h][:], scores[h][:], -0.7, bias_neg[:], ALU.mult, ALU.add)
-        for h in range(HALVES):
             nc.vector.tensor_reduce(low[h][:], neg[h][:], mybir.AxisListType.X, ALU.min)
             nc.scalar.activation(ex[h][:], neg[h][:], ACT.Exp, bias=low[h][:], scale=-1.0)
         for h in range(HALVES):
-            nc.vector.scalar_tensor_tensor(
-                e[h][:], ex[h][:], 1.0, prior[:], ALU.mult, ALU.mult, accum_out=total[:, h : h + 1]
-            )
-        nc.vector.reciprocal(inverse[:], total[:])
-        nc.vector.tensor_scalar(share[:], inverse[:], 256.0, None, ALU.mult)
+            nc.vector.scalar_tensor_tensor(e[h][:], ex[h][:], 1.0, prior[:], ALU.mult, ALU.mult, accum_out=total[h][:])
+            nc.vector.reciprocal(inverse[h][:], total[h][:])
         for h in range(HALVES):
-            nc.vector.scalar_tensor_tensor(y[h][:], e[h][:], share[:, h : h + 1], prior[:], ALU.mult, ALU.subtract)
+            nc.vector.tensor_scalar(share[h][:], inverse[h][:], 256.0, None, ALU.mult)
+        for h in range(HALVES):
+            nc.vector.scalar_tensor_tensor(y[h][:], e[h][:], share[h][:], prior[:], ALU.mult, ALU.subtract)
             nc.sync.dma_start(out[h * P : (h + 1) * P, :], y[h][:])

@@ -20,6 +20,8 @@ PACK = 4
 PASSES = K // (P * PACK)
 HALVES = J // P
 LIST_COLS = J // 16
+PAIRS = PASSES * PACK // 2
+PIECE = 64
 FK_ROW, FI_ROW, COL_ROW, SMALL_ROWS = 0, 2, 4, 5
 
 
@@ -39,8 +41,7 @@ def tile_list_scores_products_mixed_shares_f_kernel(tc, xf, xb, fk, kf, ko, fi, 
 
         ko_sb = sb.tile([P, PASSES, PACK, I], F32, name="ko_sb")
         xb_sb = [sb.tile([P, PACK, S], F32, name="xb_sb%d" % a) for a in range(PASSES)]
-        kf_first = sb.tile([P, PACK, V], F32, name="kf_first")
-        kf_last = [sb.tile([P, 2, V], F32, name="kf_last%d" % c) for c in range(2)]
+        kf_sb = [sb.tile([P, PACK, V], F32, name="kf_sb%d" % a) for a in range(PASSES)]
         xf_sb = [[sb.tile([P, T], F32, name="xf_sb%d_%d" % (a, t)) for t in range(PACK)] for a in range(PASSES)]
 
         small = sb.tile([P, P * PACK], F32, name="small")
@@ -50,14 +51,13 @@ def tile_list_scores_products_mixed_shares_f_kernel(tc, xf, xb, fk, kf, ko, fi, 
         nc.scalar.dma_start(small[COL_ROW : COL_ROW + 1, 0:I], bi)
         nc.scalar.dma_start(small[COL_ROW : COL_ROW + 1, I : 2 * I], pr)
 
-        nc.sync.dma_start(kf_first[:], rows(kf)[0])
+        nc.sync.dma_start(kf_sb[0][:], rows(kf)[0])
         nc.sync.dma_start(idx3[:], offs3)
         nc.sync.dma_start(idx2[:], offs2)
         nc.sync.dma_start(xb_sb[0][:], rows(xb)[0])
         nc.sync.dma_start(ko_sb[:], ko.rearrange("(a p t) w -> p a t w", p=P, t=PACK))
+        nc.sync.dma_start(kf_sb[1][:], rows(kf)[1])
         nc.sync.dma_start(idx[:], offs)
-        for c in range(2):
-            nc.sync.dma_start(kf_last[c][:], rows(kf)[1, :, 2 * c : 2 * c + 2, :])
         nc.sync.dma_start(xb_sb[1][:], rows(xb)[1])
         for a in range(PASSES):
             for t in range(PACK):
@@ -89,11 +89,16 @@ def tile_list_scores_products_mixed_shares_f_kernel(tc, xf, xb, fk, kf, ko, fi, 
             )
             return codes, scales
 
-        def gather_xb(a):
-            g = sb.tile([P, PACK, J], F32, name="xb_g%d" % a)
+        def make_xb_fk(a):
+            picked = sb.tile([P, PACK, J], F32, name="xb_picked%d" % a)
+            scaled = sb.tile([P, PACK, J], F32, name="xb_fk%d" % a)
             for t in range(PACK):
-                nc.scalar.activation(g[:, t, :], xb_sb[a][:, t, :].indirect(idx2[:]), ACT.Copy)
-            return g
+                nc.scalar.activation(picked[:, t, :], xb_sb[a][:, t, :].indirect(idx2[:]), ACT.Copy)
+            for t in range(PACK):
+                nc.scalar.activation(
+                    scaled[:, t, :], picked[:, t, :], ACT.Copy, scale=turned[:, t, FK_ROW + a : FK_ROW + a + 1]
+                )
+            return scaled
 
         def make_vk(a, windows):
             words = sb.tile([P, I, PACK], BF16, name="vk_words%d" % a, align_bytes=64)
@@ -105,10 +110,10 @@ def tile_list_scores_products_mixed_shares_f_kernel(tc, xf, xb, fk, kf, ko, fi, 
                 nc.vector.tensor_scalar(words[:, :, t], keys[:], turned[:, t, FI_ROW + a : FI_ROW + a + 1], None, ALU.mult)
             return quantise("vk%d" % a, words, I)
 
-        vk_q = [make_vk(0, [kf_first[:, t, :] for t in range(PACK)])]
-        xb_g = [gather_xb(0)]
-        vk_q.append(make_vk(1, [kf_last[t // 2][:, t % 2, :] for t in range(PACK)]))
-        xb_g.append(gather_xb(1))
+        vk_q = [make_vk(0, [kf_sb[0][:, t, :] for t in range(PACK)])]
+        xb_fk = [make_xb_fk(0)]
+        vk_q.append(make_vk(1, [kf_sb[1][:, t, :] for t in range(PACK)]))
+        xb_fk.append(make_xb_fk(1))
 
         scores = [ps.tile([P, I], F32, name="scores%d" % h) for h in range(HALVES)]
 
@@ -123,25 +128,40 @@ def tile_list_scores_products_mixed_shares_f_kernel(tc, xf, xb, fk, kf, ko, fi, 
                 stop=(a == PASSES - 1),
             )
 
-        for a in range(PASSES):
-            half_words = [
-                sb.tile([P, P, PACK], BF16, name="u_words%d_%d" % (a, h), align_bytes=64) for h in range(HALVES)
-            ]
-            for t in range(PACK):
-                prod = sb.tile([P, J], F32, name="prod%d_%d" % (a, t))
-                pieces = HALVES if (a, t) == (PASSES - 1, PACK - 1) else 1
-                width = J // pieces
-                for c in range(pieces):
-                    cols = slice(c * width, (c + 1) * width)
-                    picks = idx[:, c * width // 16 : (c + 1) * width // 16]
-                    nc.vector.tensor_tensor(prod[:, cols], xf_sb[a][t][:].indirect(picks), xb_g[a][:, t, cols], ALU.mult)
-                for h in range(HALVES):
-                    nc.scalar.activation(
-                        half_words[h][:, :, t], prod[:, h * P : (h + 1) * P], ACT.Copy, scale=turned[:, t, FK_ROW + a : FK_ROW + a + 1]
-                    )
+        u_words = [
+            [sb.tile([P, P, PACK], BF16, name="u_words%d_%d" % (a, h), align_bytes=64) for h in range(HALVES)]
+            for a in range(PASSES)
+        ]
+
+        def round_pair(n, u_pair, first, width):
+            a, t = n // 2, 2 * (n % 2)
+            h, c = divmod(first, P)
+            nc.scalar.copy(
+                u_words[a][h][:, c : c + width, t : t + 2],
+                u_pair[:, :, first : first + width].rearrange("p s j -> p j s"),
+            )
+
+        def finish_pass(a):
             for h in range(HALVES):
-                u_codes, u_scales = quantise("u%d_%d" % (a, h), half_words[h], P)
+                u_codes, u_scales = quantise("u%d_%d" % (a, h), u_words[a][h], P)
                 multiply(h, a, u_codes[:], u_scales[:])
+
+        for n in range(PAIRS):
+            a, t = n // 2, 2 * (n % 2)
+            u_pair = sb.tile([P, 2, J], F32, name="u_pair%d" % n)
+            nc.vector.tensor_tensor(u_pair[:, 0, :], xf_sb[a][t][:].indirect(idx[:]), xb_fk[a][:, t, :], ALU.mult)
+            width = PIECE if n == PAIRS - 1 else J
+            for first in range(0, J, width):
+                cols = slice(first, first + width)
+                picks = idx[:, first // 16 : (first + width) // 16]
+                nc.vector.tensor_tensor(
+                    u_pair[:, 1, cols], xf_sb[a][t + 1][:].indirect(picks), xb_fk[a][:, t + 1, cols], ALU.mult
+                )
+            width = min(width, P)
+            for first in range(0, J, width):
+                round_pair(n, u_pair, first, width)
+            if t + 2 == PACK:
+                finish_pass(a)
 
         neg = [sb.tile([P, I], F32, name="neg%d" % h) for h in range(HALVES)]
         low = [sb.tile([P, 1], F32, name="low%d" % h) for h in range(HALVES)]

from contextlib import ExitStack

import concourse.mybir as mybir
from concourse.masks import make_identity

K, T, J, I, S, V = 1024, 1024, 256, 256, 512, 1024
FLOPS = 2 * K * J * I

F32 = mybir.dt.float32
BF16 = mybir.dt.bfloat16
U32 = mybir.dt.uint32
U16 = mybir.dt.uint16
U8 = mybir.dt.uint8
E5M2X4 = mybir.dt.float8_e5m2_x4
ALU = mybir.AluOpType
ACT = mybir.ActivationFunctionType

P = 128
PACK = 4
PASSES = K // (P * PACK)
HALVES = J // P
LIST_COLS = J // 16
PAIRS = PASSES * PACK // 2
PIECE = 64
FK_ROW, FI_ROW, COL_ROW, SMALL_ROWS = 0, 2, 4, 5


def tile_list_scores_products_mixed_shares_f_kernel(tc, xf, xb, fk, kf, ko, fi, bi, pr, offs, offs2, offs3, out):
    nc = tc.nc
    with ExitStack() as ctx:
        lists = ctx.enter_context(tc.tile_pool(name="lists", bufs=1))
        sb = ctx.enter_context(tc.tile_pool(name="sb", bufs=1))
        ps = ctx.enter_context(tc.psum_pool(name="ps", bufs=1))

        def rows(x):
            return x.rearrange("(a p t) w -> a p t w", p=P, t=PACK)

        idx = lists.tile([P, LIST_COLS], U16, name="idx")
        idx2 = lists.tile([P, LIST_COLS], U16, name="idx2")
        idx3 = lists.tile([P, LIST_COLS], U16, name="idx3")

        ko_sb = sb.tile([P, PASSES, PACK, I], F32, name="ko_sb")
        xb_sb = [sb.tile([P, PACK, S], F32, name="xb_sb%d" % a) for a in range(PASSES)]
        kf_sb = [sb.tile([P, PACK, V], F32, name="kf_sb%d" % a) for a in range(PASSES)]
        xf_sb = [[sb.tile([P, T], F32, name="xf_sb%d_%d" % (a, t)) for t in range(PACK)] for a in range(PASSES)]

        small = sb.tile([P, P * PACK], F32, name="small")
        nc.vector.memset(small[:], 0.0)
        nc.scalar.dma_start(small[FK_ROW : FK_ROW + PASSES, :], fk.rearrange("(a r) o -> a (r o)", a=PASSES))
        nc.scalar.dma_start(small[FI_ROW : FI_ROW + PASSES, :], fi.rearrange("(a r) o -> a (r o)", a=PASSES))
        nc.scalar.dma_start(small[COL_ROW : COL_ROW + 1, 0:I], bi)
        nc.scalar.dma_start(small[COL_ROW : COL_ROW + 1, I : 2 * I], pr)

        nc.sync.dma_start(kf_sb[0][:], rows(kf)[0])
        nc.sync.dma_start(idx3[:], offs3)
        nc.sync.dma_start(idx2[:], offs2)
        nc.sync.dma_start(xb_sb[0][:], rows(xb)[0])
        nc.sync.dma_start(ko_sb[:], ko.rearrange("(a p t) w -> p a t w", p=P, t=PACK))
        nc.sync.dma_start(kf_sb[1][:], rows(kf)[1])
        nc.sync.dma_start(idx[:], offs)
        nc.sync.dma_start(xb_sb[1][:], rows(xb)[1])
        for a in range(PASSES):
            for t in range(PACK):
                nc.sync.dma_start(xf_sb[a][t][:], rows(xf)[a, :, t, :])

        ident = sb.tile([P, P], F32, name="ident")
        make_identity(nc, ident[:])
        turned_ps = ps.tile([P, PACK, P], F32, name="turned_ps")
        for t in range(PACK):
            nc.tensor.transpose(turned_ps[:, t, :], small[:, t :: PACK], ident[:])
        turned = sb.tile([P, PACK, SMALL_ROWS], F32, name="turned")
        nc.vector.tensor_copy(turned[:], turned_ps[:, :, 0:SMALL_ROWS])
        spread_ps = ps.tile([P, PACK, P], F32, name="spread_ps")
        for t in range(PACK):
            nc.tensor.transpose(spread_ps[:, t, :], turned[:, t, COL_ROW : COL_ROW + 1].to_broadcast([P, P]), ident[:])
        bias_neg = sb.tile([P, I], F32, name="bias_neg")
        prior = sb.tile([P, I], F32, name="prior")
        by_column = spread_ps[:].rearrange("p t q -> p q t")
        nc.vector.tensor_scalar(
            bias_neg[:].rearrange("p (q t) -> p q t", t=PACK), by_column[:, 0 : I // PACK, :], -0.7, None, ALU.mult
        )
        nc.vector.tensor_copy(prior[:].rearrange("p (q t) -> p q t", t=PACK), by_column[:, I // PACK : P, :])

        def quantise(name, words, width):
            codes = sb.tile([P, width], U32, name=name + "_codes", align_bytes=64)
            scales = sb.tile([P, width], U8, name=name + "_scales", align_bytes=64)
            nc.vector.quantize_mx(
                out=codes[:].bitcast(E5M2X4), scales=scales[:], in_=words[:].rearrange("p w t -> p (w t)")
            )
            return codes, scales

        def make_xb_fk(a):
            picked = sb.tile([P, PACK, J], F32, name="xb_picked%d" % a)
            scaled = sb.tile([P, PACK, J], F32, name="xb_fk%d" % a)
            for t in range(PACK):
                nc.scalar.activation(picked[:, t, :], xb_sb[a][:, t, :].indirect(idx2[:]), ACT.Copy)
            for t in range(PACK):
                nc.scalar.activation(
                    scaled[:, t, :], picked[:, t, :], ACT.Copy, scale=turned[:, t, FK_ROW + a : FK_ROW + a + 1]
                )
            return scaled

        def make_vk(a, windows):
            words = sb.tile([P, I, PACK], BF16, name="vk_words%d" % a, align_bytes=64)
            for t in range(PACK):
                g = sb.tile([P, I], F32, name="kf_g%d_%d" % (a, t))
                nc.scalar.activation(g[:], windows[t].indirect(idx3[:]), ACT.Copy)
                keys = sb.tile([P, I], F32, name="keys%d_%d" % (a, t))
                nc.vector.tensor_tensor(keys[:], g[:], ko_sb[:, a, t, :], ALU.add)
                nc.vector.tensor_scalar(words[:, :, t], keys[:], turned[:, t, FI_ROW + a : FI_ROW + a + 1], None, ALU.mult)
            return quantise("vk%d" % a, words, I)

        vk_q = [make_vk(0, [kf_sb[0][:, t, :] for t in range(PACK)])]
        xb_fk = [make_xb_fk(0)]
        vk_q.append(make_vk(1, [kf_sb[1][:, t, :] for t in range(PACK)]))
        xb_fk.append(make_xb_fk(1))

        scores = [ps.tile([P, I], F32, name="scores%d" % h) for h in range(HALVES)]

        def multiply(h, a, u_codes, u_scales):
            nc.tensor.matmul_mx(
                out=scores[h][:],
                lhsT=u_codes.bitcast(E5M2X4),
                lhsT_scale=u_scales,
                rhs=vk_q[a][0][:].bitcast(E5M2X4),
                rhs_scale=vk_q[a][1][:],
                start=(a == 0),
                stop=(a == PASSES - 1),
            )

        u_words = [
            [sb.tile([P, P, PACK], BF16, name="u_words%d_%d" % (a, h), align_bytes=64) for h in range(HALVES)]
            for a in range(PASSES)
        ]

        def round_pair(n, u_pair, first, width):
            a, t = n // 2, 2 * (n % 2)
            h, c = divmod(first, P)
            nc.scalar.copy(
                u_words[a][h][:, c : c + width, t : t + 2],
                u_pair[:, :, first : first + width].rearrange("p s j -> p j s"),
            )

        def finish_pass(a):
            for h in range(HALVES):
                u_codes, u_scales = quantise("u%d_%d" % (a, h), u_words[a][h], P)
                multiply(h, a, u_codes[:], u_scales[:])

        for n in range(PAIRS):
            a, t = n // 2, 2 * (n % 2)
            u_pair = sb.tile([P, 2, J], F32, name="u_pair%d" % n)
            nc.vector.tensor_tensor(u_pair[:, 0, :], xf_sb[a][t][:].indirect(idx[:]), xb_fk[a][:, t, :], ALU.mult)
            width = PIECE if n == PAIRS - 1 else J
            for first in range(0, J, width):
                cols = slice(first, first + width)
                picks = idx[:, first // 16 : (first + width) // 16]
                nc.vector.tensor_tensor(
                    u_pair[:, 1, cols], xf_sb[a][t + 1][:].indirect(picks), xb_fk[a][:, t + 1, cols], ALU.mult
                )
            width = min(width, P)
            for first in range(0, J, width):
                round_pair(n, u_pair, first, width)
            if t + 2 == PACK:
                finish_pass(a)

        neg = [sb.tile([P, I], F32, name="neg%d" % h) for h in range(HALVES)]
        low = [sb.tile([P, 1], F32, name="low%d" % h) for h in range(HALVES)]
        ex = [sb.tile([P, I], F32, name="ex%d" % h) for h in range(HALVES)]
        e = [sb.tile([P, I], F32, name="e%d" % h) for h in range(HALVES)]
        y = [sb.tile([P, I], F32, name="y%d" % h) for h in range(HALVES)]
        total = [sb.tile([P, 1], F32, name="total%d" % h) for h in range(HALVES)]
        inverse = [sb.tile([P, 1], F32, name="inverse%d" % h) for h in range(HALVES)]
        share = [sb.tile([P, 1], F32, name="share%d" % h) for h in range(HALVES)]
        for h in range(HALVES):
            nc.vector.scalar_tensor_tensor(neg[h][:], scores[h][:], -0.7, bias_neg[:], ALU.mult, ALU.add)
            nc.vector.tensor_reduce(low[h][:], neg[h][:], mybir.AxisListType.X, ALU.min)
            nc.scalar.activation(ex[h][:], neg[h][:], ACT.Exp, bias=low[h][:], scale=-1.0)
        for h in range(HALVES):
            nc.vector.scalar_tensor_tensor(e[h][:], ex[h][:], 1.0, prior[:], ALU.mult, ALU.mult, accum_out=total[h][:])
            nc.vector.reciprocal(inverse[h][:], total[h][:])
        for h in range(HALVES):
            nc.vector.tensor_scalar(share[h][:], inverse[h][:], 256.0, None, ALU.mult)
        for h in range(HALVES):
            nc.vector.scalar_tensor_tensor(y[h][:], e[h][:], share[h][:], prior[:], ALU.mult, ALU.subtract)
            nc.sync.dma_start(out[h * P : (h + 1) * P, :], y[h][:])
